import numpy as np
import ml_dtypes


def mxq(x, axis, fmt="e4m3"):
    dtype, down = {"e4m3": (ml_dtypes.float8_e4m3fn, 7), "e5m2": (ml_dtypes.float8_e5m2, 14)}[fmt]
    v = np.moveaxis(np.asarray(x, np.float32).astype(ml_dtypes.bfloat16).astype(np.float64), axis, -1)
    blocks = v.reshape(v.shape[:-1] + (-1, 32))
    amax = np.abs(blocks).max(-1, keepdims=True)
    byte = np.maximum(np.where(amax > 0, np.frexp(amax)[1] - 1 + 127, 0) - down, 1)
    scale = np.exp2(byte - 127.0)
    codes = (blocks / scale).astype(np.float32).astype(dtype).astype(np.float64)
    return np.moveaxis((codes * scale).reshape(v.shape), -1, axis)


WIDE = False


def mx_kscale(k):
    if not WIDE:
        return np.ones(k)
    levels = np.array([10, -10, 5, -5, 0])
    if k % 512:
        return np.exp2(np.random.permutation(np.resize(levels, k // 32))).repeat(32)
    a = np.empty((k // 512, 16))
    for p in range(k // 512):
        a[p, :8] = np.random.permutation(np.resize(levels, 8))
        for g in range(8):
            far = levels[np.abs(levels - a[p, g]) >= 10]
            a[p, g + 8] = far[np.random.randint(len(far))]
    return np.exp2(a.ravel()).repeat(32)


def f64(x):
    return np.asarray(x).astype(np.float64)


def striped(idx):
    return np.tile(idx.reshape(-1, 16).T, (8, 1)).astype(np.uint16)


def unstriped(offs):
    return offs[:16].T.reshape(-1).astype(np.int64)


def striped8(idx):
    return np.concatenate([x.reshape(-1, 16).T for x in idx]).astype(np.uint16)


def runs(offs, k):
    lists = np.stack([offs[16 * r : 16 * r + 16].T.reshape(-1) for r in range(8)]).astype(np.int64)
    return lists[np.arange(k) % 512 // 64]


def pack_weight(w):
    k, n = w.shape
    w = f64(np.asarray(w, np.float32).astype(ml_dtypes.bfloat16)).reshape(k // 32, 32, n)
    amax = np.abs(w).max(1)
    byte = np.clip(np.where(amax > 0, np.frexp(amax)[1] - 1 + 127 - 7, 1), 1, 254)
    scaled = (w * np.exp2(127.0 - byte)[:, None, :]).reshape(k, n).astype(np.float32)
    words = np.ascontiguousarray(scaled.reshape(k // 512, 128, 4, n).transpose(0, 1, 3, 2)).astype(ml_dtypes.float8_e4m3fn).view(np.uint8)
    return words, np.ascontiguousarray(byte.astype(np.uint8).reshape(k // 512, 16, n))


def unpack_weight(words, scales):
    g, p, n, _ = words.shape
    vals = np.ascontiguousarray(words).view(ml_dtypes.float8_e4m3fn).astype(np.float64) * np.repeat(np.exp2(scales.astype(np.float64) - 127.0), 8, axis=1)[..., None]
    return vals.transpose(0, 1, 3, 2).reshape(g * 512, n)


E2M1 = np.array([0.0, 0.5, 1.0, 1.5, 2.0, 3.0, 4.0, 6.0, -0.0, -0.5, -1.0, -1.5, -2.0, -3.0, -4.0, -6.0])


def pack_fp4(w):
    k, n = w.shape
    w = f64(np.asarray(w, np.float32).astype(ml_dtypes.bfloat16)).reshape(k // 32, 32, n)
    amax = np.abs(w).max(1)
    mant, ex = np.frexp(amax / 6.0)
    byte = np.clip(np.where(amax > 0, np.where(mant > 0.5, ex, ex - 1) + 127, 1), 1, 254)
    scaled = (w * np.exp2(127.0 - byte)[:, None, :]).reshape(k, n).astype(np.float32)
    c = np.ascontiguousarray(scaled.reshape(k // 512, 128, 4, n).transpose(0, 1, 3, 2)).astype(ml_dtypes.float4_e2m1fn).view(np.uint8) & 0xF
    words = (c[..., 0::2] | (c[..., 1::2] << 4)).reshape(k // 512, 128, 2 * n)
    return np.ascontiguousarray(words), np.ascontiguousarray(byte.astype(np.uint8).reshape(k // 512, 16, n))


def unpack_fp4(words, scales):
    g, _, n = scales.shape
    words = np.ascontiguousarray(words).reshape(g, 128, n, 2)
    nib = np.empty((g, 128, n, 4), np.uint8)
    nib[..., 0::2] = words & 0xF
    nib[..., 1::2] = words >> 4
    vals = E2M1[nib] * np.repeat(np.exp2(scales.astype(np.float64) - 127.0), 8, axis=1)[..., None]
    return vals.transpose(0, 1, 3, 2).reshape(g * 512, n)


def planes(y):
    n, m = y.shape
    v = y.astype(np.float32).astype(ml_dtypes.bfloat16).astype(np.float64).reshape(n // 32, 32, m)
    top = np.abs(v).max(1)
    byte = np.clip(np.where(top > 0, np.frexp(top)[1] - 1 + 127 - 7, 1), 1, 254)
    codes = (v * np.exp2(127.0 - byte)[:, None, :]).reshape(n, m).astype(np.float32).astype(ml_dtypes.float8_e4m3fn).view(np.uint8)
    words = codes.reshape(n // 512, 128, 4, m).transpose(0, 1, 3, 2)
    return np.ascontiguousarray(words), np.ascontiguousarray(byte.astype(np.uint8).reshape(n // 512, 16, m))


K, T, S, V, N, H, W, U = 512, 2048, 512, 512, 512, 512, 256, 1024


def setup_inputs():
    n = np.random.standard_normal
    s = mx_kscale(K)[:, None]
    u = mx_kscale(S)
    packed_xT = pack_weight(n((K, T)) * s)
    packed_w1 = pack_fp4(n((K, H)) / np.sqrt(K) / s)
    packed_w2 = pack_fp4(n((K, H)) / np.sqrt(K) / s)
    packed_w3 = pack_fp4(n((S, N)) / np.sqrt(S) / u[:, None])
    perm = np.stack([np.random.permutation(S) for _ in range(8)])
    return {
        "x_words": packed_xT[0],
        "x_scales": packed_xT[1],
        "w1_words": packed_w1[0],
        "w1_scales": packed_w1[1],
        "w2_words": packed_w2[0],
        "w2_scales": packed_w2[1],
        "ga": (np.random.uniform(0.5, 1.5, (H, 1)) * u[:, None]).astype(np.float32),
        "gb": (np.random.uniform(0.5, 1.5, (H, 1)) / u[:, None]).astype(np.float32),
        "mem": n((S, U)).astype(np.float32),
        "gt": (np.random.uniform(0.5, 1.5, (S, 1)) * u[:, None]).astype(np.float32),
        "res": (1.5 * n((N, U))).astype(np.float32),
        "w3_words": packed_w3[0],
        "w3_scales": packed_w3[1],
        "offs": striped(np.random.permutation(T)[:S]),
        "two": striped(np.random.permutation(T)[:V]),
        "n1": striped8(perm[:, :W]),
        "n2": striped8(perm[:, W:]),
        "n3": striped8(np.stack([np.random.permutation(U)[:V] for _ in range(8)])),
    }


def reference(x_words, x_scales, w1_words, w1_scales, w2_words, w2_scales, ga, gb, mem, gt, res, w3_words, w3_scales, offs, two, n1, n2, n3):
    xq = unpack_weight(x_words, x_scales)[:, unstriped(offs)]
    a = unpack_fp4(w1_words, w1_scales).T @ xq
    pa = a[np.arange(H)[:, None], runs(n1, H)]
    pb = a[np.arange(H)[:, None], runs(n2, H)]
    rb = np.maximum(0.5 * pa, pb)
    ra = pb - pa
    ds = np.zeros((H, S))
    ds[np.arange(H)[:, None], runs(n1, H)] = ra
    dt = ds.copy()
    dt[np.arange(H)[:, None], runs(n2, H)] = rb
    z = f64(ga) * dt
    x_two = unpack_weight(x_words, x_scales)[:, unstriped(two)]
    b = unpack_fp4(w2_words, w2_scales).T @ x_two
    z2 = f64(gb) * b
    s = 0.0625 * ((mxq(z, 0, "e4m3").T @ mxq(z2, 0, "e4m3")))
    nw = np.maximum(s, 0.5 * (f64(mem)[np.arange(S)[:, None], runs(n3, S)]))
    pg = f64(mem).copy()
    pg[np.arange(S)[:, None], runs(n3, S)] = nw
    z3 = f64(gt) * pg
    out_0 = f64(res) + (unpack_fp4(w3_words, w3_scales).T @ mxq(z3, 0, "e4m3"))
    return (out_0,) + planes(out_0)

@@ -1,0 +1,293 @@
+from contextlib import ExitStack
+
+import concourse.mybir as mybir
+from concourse.masks import make_identity
+
+K, T, S, V, N, H, W, U = 512, 2048, 512, 512, 512, 512, 256, 1024
+FLOPS = 2 * (K * H * S + K * H * V + H * S * V + S * N * U)
+
+F32 = mybir.dt.float32
+BF16 = mybir.dt.bfloat16
+I32 = mybir.dt.int32
+U32 = mybir.dt.uint32
+U16 = mybir.dt.uint16
+U8 = mybir.dt.uint8
+FP8X4 = mybir.dt.float8_e4m3fn_x4
+FP4X4 = mybir.dt.float4_e2m1fn_x4
+ALU = mybir.AluOpType
+COPY = mybir.ActivationFunctionType.Copy
+
+P = 128
+PACK = 4
+CHUNKS = (128, 256, 256, 128, 128, 128)
+VECTOR_ROUNDS_FROM = 4
+EARLY_CODES = 3
+
+
+def tile_picked_valliftpagex_none_po_kernel(
+    tc, x_words, x_scales, w1_words, w1_scales, w2_words, w2_scales, ga, gb, mem, gt, res,
+    w3_words, w3_scales, offs, two, n1, n2, n3, out_0, out_1, out_2
+):
+    nc = tc.nc
+    with ExitStack() as ctx:
+        lists = ctx.enter_context(tc.tile_pool(name="lists", bufs=1))
+        sb = ctx.enter_context(tc.tile_pool(name="sb", bufs=1))
+        psum = ctx.enter_context(tc.psum_pool(name="psum", bufs=1))
+
+        def tile(name, shape, dtype, tag=None):
+            return sb.tile(shape, dtype, name=name, tag=tag or name, align_bytes=64)
+
+        def bank(index, name, shape):
+            return psum.tile(shape, F32, name=name, tag="bank%d" % index)
+
+        def load_list(name, source):
+            held = lists.tile([P, source.shape[1]], U16, name=name)
+            nc.sync.dma_start(held[:], source)
+            return held
+
+        def load_scale_rows(plane, source):
+            for quad in range(4):
+                nc.sync.dma_start(
+                    plane[32 * quad : 32 * quad + 4, :].bitcast(I32),
+                    source[0, 4 * quad : 4 * quad + 4, :].bitcast(I32),
+                )
+
+        def load_fp4_words(name, source):
+            held = tile(name, [P, 2 * H], U8)
+            nc.sync.dma_start(held[:].bitcast(I32), source[0].bitcast(I32))
+            return held
+
+        x_scale_table = tile("x_scale_table", [P, T], U8)
+        nc.vector.memset(x_scale_table[:].bitcast(I32), 0)
+        raw_scales = []
+        for i in range(3):
+            plane = tile("raw_scales%d" % i, [P, H], U8)
+            (nc.vector if i == 0 else nc.gpsimd).memset(plane[:].bitcast(I32), 0)
+            raw_scales.append(plane)
+        identity = tile("identity", [P, P], F32)
+        gain_rows = tile("gain_rows", [P, P], F32)
+        nc.gpsimd.memset(gain_rows[:], 0.0)
+        make_identity(nc, identity[:])
+
+        offs_list = load_list("offs_list", offs)
+        two_list = load_list("two_list", two)
+        w1_raw = load_fp4_words("w1_raw", w1_words)
+        load_scale_rows(x_scale_table, x_scales)
+        x_word_table = tile("x_word_table", [P, T], I32)
+        nc.sync.dma_start(x_word_table[:], x_words[0].rearrange("p n t -> p (n t)").bitcast(I32))
+        load_scale_rows(raw_scales[0], w1_scales)
+        n1_list = load_list("n1_list", n1)
+        n2_list = load_list("n2_list", n2)
+        w2_raw = load_fp4_words("w2_raw", w2_words)
+        load_scale_rows(raw_scales[1], w2_scales)
+        for i, gain in enumerate((ga, gb)):
+            nc.sync.dma_start(
+                gain_rows[4 * i : 4 * i + 4, :].rearrange("t (q r) -> t q r", r=8),
+                gain.rearrange("(q t r) o -> t q (r o)", t=PACK, r=8),
+            )
+        n3_list = load_list("n3_list", n3)
+        mem_rows = mem.rearrange("(p t) w -> t p w", t=PACK)
+        page = []
+        for t in range(PACK):
+            rows = tile("page%d" % t, [P, U], F32)
+            nc.sync.dma_start(rows[:], mem_rows[t])
+            page.append(rows)
+        gt_cols = tile("gt_cols", [P, PACK], F32)
+        nc.sync.dma_start(gt_cols[:], gt.rearrange("(p t) o -> p (t o)", t=PACK))
+        w3_raw = load_fp4_words("w3_raw", w3_words)
+        load_scale_rows(raw_scales[2], w3_scales)
+        res_rows = res.rearrange("(p t) w -> p t w", t=PACK)
+        out_rows = out_0.rearrange("(p t) w -> p t w", t=PACK)
+        starts = [sum(CHUNKS[:c]) for c in range(len(CHUNKS))]
+        residual = []
+        for c, width in enumerate(CHUNKS):
+            part = tile("residual%d" % c, [P, PACK, width], F32)
+            nc.sync.dma_start(part[:], res_rows[:, :, starts[c] : starts[c] + width])
+            residual.append(part)
+
+        def pick_scales(name, offsets):
+            picked = tile(name, [P, S], U8)
+            nc.vector.tensor_copy(picked[:], x_scale_table[:].indirect(offsets[:]))
+            return picked
+
+        def pick_words(name, offsets):
+            picked = tile(name, [P, S], U32)
+            nc.vector.tensor_copy(picked[:], x_word_table[:].bitcast(U32).indirect(offsets[:]))
+            return picked
+
+        def deal_by_eights(name, raw, run):
+            dealt = tile(name, list(raw.shape), U8)
+            nc.vector.tensor_copy(
+                dealt[:].bitcast(I32).rearrange("p (t q r) -> p t q r", t=PACK, r=run),
+                raw[:].bitcast(I32).rearrange("p (q t r) -> p t q r", t=PACK, r=run),
+            )
+            return dealt
+
+        def deal_by_ones(name, raw, run):
+            dealt = tile(name, list(raw.shape), U8)
+            nc.vector.tensor_copy(
+                dealt[:].rearrange("p (t m r) -> p t m r", t=PACK, r=run),
+                raw[:].rearrange("p (m t r) -> p t m r", t=PACK, r=run),
+            )
+            return dealt
+
+        def weight_pass(acc, words, scales, t, codes, code_scales):
+            nc.tensor.matmul_mx(
+                out=acc,
+                lhsT=words[:, 2 * P * t : 2 * P * (t + 1)].bitcast(FP4X4),
+                lhsT_scale=scales[:, P * t : P * (t + 1)],
+                rhs=codes.bitcast(FP8X4),
+                rhs_scale=code_scales,
+                start=True,
+                stop=True,
+            )
+
+        def quantize(codes, scales, grouped):
+            nc.vector.quantize_mx(out=codes.bitcast(FP8X4), scales=scales, in_=grouped)
+
+        xa_scales = pick_scales("xa_scales", offs_list)
+        xb_scales = pick_scales("xb_scales", two_list)
+        w1_dealt = deal_by_eights("w1_dealt", w1_raw, 4)
+        xa_words = pick_words("xa_words", offs_list)
+        w1_dealt_scales = deal_by_eights("w1_dealt_scales", raw_scales[0], 2)
+        xb_words = pick_words("xb_words", two_list)
+        w2_dealt = deal_by_eights("w2_dealt", w2_raw, 4)
+        w2_dealt_scales = deal_by_eights("w2_dealt_scales", raw_scales[1], 2)
+
+        a_rows = []
+        for t in range(PACK):
+            acc = bank(t, "a_acc%d" % t, [P, S])
+            weight_pass(acc[:], w1_dealt, w1_dealt_scales, t, xa_words[:], xa_scales[:])
+            rows = tile("a_rows%d" % t, [P, S], F32)
+            nc.scalar.activation(rows[:], acc[:], COPY)
+            a_rows.append(rows)
+
+        turned = bank(7, "turned", [P, P])
+        nc.tensor.transpose(turned[:], gain_rows[:], identity[:])
+        gains = tile("gains", [P, 2 * PACK], F32)
+        nc.scalar.activation(gains[:], turned[:, 0 : 2 * PACK], COPY)
+
+        z2_grouped = tile("z2_grouped", [P, V, PACK], BF16)
+        for t in range(PACK):
+            acc = bank(PACK + t, "b_acc%d" % t, [P, V])
+            weight_pass(acc[:], w2_dealt, w2_dealt_scales, t, xb_words[:], xb_scales[:])
+            nc.scalar.activation(z2_grouped[:, :, t], acc[:], COPY, scale=gains[:, PACK + t : PACK + t + 1])
+
+        z_grouped = tile("z_grouped", [P, PACK, P, PACK], BF16)
+        lifted = []
+        for t in range(PACK):
+            neg_pa = tile("neg_pa%d" % t, [P, W], F32)
+            pb = tile("pb%d" % t, [P, W], F32)
+            rb = tile("rb%d" % t, [P, W], F32)
+            dt = tile("dt%d" % t, [P, S], F32)
+            nc.vector.tensor_scalar(neg_pa[:], a_rows[t][:].indirect(n1_list[:]), -1.0, 0.0, ALU.mult, ALU.add)
+            nc.vector.tensor_copy(pb[:], a_rows[t][:].indirect(n2_list[:]))
+            nc.vector.scalar_tensor_tensor(rb[:], neg_pa[:], -0.5, pb[:], ALU.mult, ALU.max)
+            nc.vector.tensor_tensor(dt[:].indirect(n1_list[:]), pb[:], neg_pa[:], ALU.add)
+            nc.vector.tensor_copy(dt[:].indirect(n2_list[:]), rb[:])
+            lifted.append(dt)
+            if t < PACK - 1:
+                nc.scalar.activation(
+                    z_grouped[:, :, :, t].rearrange("p u m -> p m u"),
+                    dt[:].rearrange("p (m u) -> p m u", u=PACK),
+                    COPY,
+                    scale=gains[:, t : t + 1],
+                )
+
+        z2_codes = tile("z2_codes", [P, V], U32)
+        z2_scales = tile("z2_scales", [P, V], U8)
+        quantize(z2_codes[:], z2_scales[:], z2_grouped[:].rearrange("p v t -> p (v t)"))
+
+        held_early = tile("held_early", [P, 2, V], F32, tag="rb%d" % (PACK - 1))
+        held_late = tile("held_late", [P, 2, V], F32)
+        held = [held_early[:, 0, :], held_early[:, 1, :], held_late[:, 0, :], held_late[:, 1, :]]
+
+        def fetch_held(u):
+            nc.vector.tensor_scalar(held[u], page[u][:].indirect(n3_list[:]), 0.5, 0.0, ALU.mult, ALU.add)
+
+        fetch_held(0)
+        fetch_held(1)
+
+        last = PACK - 1
+        s_acc = []
+        for u in range(PACK):
+            nc.scalar.activation(
+                z_grouped[:, u, :, last],
+                lifted[last][:].rearrange("p (m u) -> p u m", u=PACK)[:, u, :],
+                COPY,
+                scale=gains[:, last : last + 1],
+            )
+            z_codes = tile("z_codes%d" % u, [P, P], U32)
+            z_scales = tile("z_scales%d" % u, [P, P], U8)
+            quantize(z_codes[:], z_scales[:], z_grouped[:, u].rearrange("p m t -> p (m t)"))
+            acc = bank(u, "s_acc%d" % u, [P, V])
+            nc.tensor.matmul_mx(
+                out=acc[:],
+                lhsT=z_codes[:].bitcast(FP8X4),
+                lhsT_scale=z_scales[:],
+                rhs=z2_codes[:].bitcast(FP8X4),
+                rhs_scale=z2_scales[:],
+                start=True,
+                stop=True,
+            )
+            s_acc.append(acc)
+
+        z3_grouped = [tile("z3_grouped%d" % c, [P, width, PACK], BF16) for c, width in enumerate(CHUNKS)]
+        for u in range(PACK):
+            if u >= 2:
+                fetch_held(u)
+            nw = tile("nw%d" % u, [P, V], F32)
+            nc.vector.scalar_tensor_tensor(nw[:], s_acc[u][:], 0.0625, held[u], ALU.mult, ALU.max)
+            nc.vector.tensor_copy(page[u][:].indirect(n3_list[:]), nw[:])
+            if u == 0:
+                w3_dealt = deal_by_ones("w3_dealt", w3_raw, 2)
+                w3_dealt_scales = deal_by_ones("w3_dealt_scales", raw_scales[2], 1)
+            for c, width in enumerate(CHUNKS):
+                nc.scalar.activation(
+                    z3_grouped[c][:, :, u],
+                    page[u][:, starts[c] : starts[c] + width],
+                    COPY,
+                    scale=gt_cols[:, u : u + 1],
+                )
+
+        out_codes = tile("out_codes", [P, U], U32)
+        out_scales = tile("out_scales", [P, U], U8)
+        out_words = out_1[0].rearrange("p n t -> p (n t)").bitcast(I32)
+        next_bank = PACK
+        for c, width in enumerate(CHUNKS):
+            cols = slice(starts[c], starts[c] + width)
+            z3_codes = tile("z3_codes%d" % c, [P, width], U32)
+            z3_scales = tile("z3_scales%d" % c, [P, width], U8)
+            quantize(z3_codes[:], z3_scales[:], z3_grouped[c][:].rearrange("p w t -> p (w t)"))
+            result = tile("result%d" % c, [P, PACK, width], F32)
+            per_bank = 512 // width
+            for first in range(0, PACK, per_bank):
+                acc = bank(next_bank % 8, "out_acc%d_%d" % (c, first), [P, per_bank, width])
+                next_bank = next_bank + 1
+                for j in range(per_bank):
+                    weight_pass(acc[:, j, :], w3_dealt, w3_dealt_scales, first + j, z3_codes[:], z3_scales[:])
+                nc.vector.tensor_tensor(
+                    result[:, first : first + per_bank, :], acc[:], residual[c][:, first : first + per_bank, :], ALU.add
+                )
+            nc.sync.dma_start(out_rows[:, :, cols], result[:])
+            out_grouped = tile("out_grouped%d" % c, [P, width, PACK], BF16)
+            if c < VECTOR_ROUNDS_FROM:
+                nc.scalar.copy(
+                    out_grouped[:].rearrange("p (g i) t -> p g t i", i=4),
+                    result[:].rearrange("p t (g i) -> p g t i", i=4),
+                )
+            else:
+                nc.vector.tensor_copy(
+                    out_grouped[:].rearrange("p (g i) t -> p g t i", i=4),
+                    result[:].rearrange("p t (g i) -> p g t i", i=4),
+                )
+            quantize(out_codes[:, cols], out_scales[:, cols], out_grouped[:].rearrange("p w t -> p (w t)"))
+            if c == EARLY_CODES - 1:
+                nc.sync.dma_start(out_words[:, 0 : cols.stop], out_codes[:, 0 : cols.stop].bitcast(I32))
+        late = slice(starts[EARLY_CODES], U)
+        nc.sync.dma_start(out_words[:, late], out_codes[:, late].bitcast(I32))
+        for quad in range(4):
+            (nc.sync if quad % 2 else nc.scalar).dma_start(
+                out_2[0, 4 * quad : 4 * quad + 4, :].bitcast(I32),
+                out_scales[32 * quad : 32 * quad + 4, :].bitcast(I32),
+            )

@@ -16,11 +16,13 @@ FP8X4 = mybir.dt.float8_e4m3fn_x4
 FP4X4 = mybir.dt.float4_e2m1fn_x4
 ALU = mybir.AluOpType
 COPY = mybir.ActivationFunctionType.Copy
+RELU = mybir.ActivationFunctionType.Relu
 
 P = 128
 PACK = 4
-CHUNKS = (128, 256, 256, 128, 128, 128)
-VECTOR_ROUNDS_FROM = 4
+CHUNKS = (128, 128, 256, 256, 128, 128)
+Z3_CHUNKS = (128, 128, 256, 256, 256)
+VECTOR_ROUNDS_FROM = 5
 EARLY_CODES = 3
 
 
@@ -58,7 +60,8 @@ def tile_picked_valliftpagex_none_po_kernel(
             return held
 
         x_scale_table = tile("x_scale_table", [P, T], U8)
-        nc.vector.memset(x_scale_table[:].bitcast(I32), 0)
+        nc.vector.memset(x_scale_table[:].bitcast(I32)[:, 0:352], 0)
+        nc.gpsimd.memset(x_scale_table[:].bitcast(I32)[:, 352:512], 0)
         raw_scales = []
         for i in range(3):
             plane = tile("raw_scales%d" % i, [P, H], U8)
@@ -117,14 +120,14 @@ def tile_picked_valliftpagex_none_po_kernel(
 
         def deal_by_eights(name, raw, run):
             dealt = tile(name, list(raw.shape), U8)
-            nc.vector.tensor_copy(
+            nc.gpsimd.tensor_copy(
                 dealt[:].bitcast(I32).rearrange("p (t q r) -> p t q r", t=PACK, r=run),
                 raw[:].bitcast(I32).rearrange("p (q t r) -> p t q r", t=PACK, r=run),
             )
             return dealt
 
-        def deal_by_ones(name, raw, run):
-            dealt = tile(name, list(raw.shape), U8)
+        def deal_by_ones(name, raw, run, tag):
+            dealt = tile(name, list(raw.shape), U8, tag=tag)
             nc.vector.tensor_copy(
                 dealt[:].rearrange("p (t m r) -> p t m r", t=PACK, r=run),
                 raw[:].rearrange("p (m t r) -> p t m r", t=PACK, r=run),
@@ -173,7 +176,23 @@ def tile_picked_valliftpagex_none_po_kernel(
             weight_pass(acc[:], w2_dealt, w2_dealt_scales, t, xb_words[:], xb_scales[:])
             nc.scalar.activation(z2_grouped[:, :, t], acc[:], COPY, scale=gains[:, PACK + t : PACK + t + 1])
 
-        z_grouped = tile("z_grouped", [P, PACK, P, PACK], BF16)
+        half_page = []
+        for u in range(PACK):
+            half = tile("half_page%d" % u, [P, U], F32)
+            nc.scalar.activation(half[:], page[u][:], COPY, scale=0.5)
+            half_page.append(half)
+
+        last = PACK - 1
+        z_grouped = [tile("z_grouped%d" % u, [P, P, PACK], BF16) for u in range(PACK)]
+
+        def round_z(t, u):
+            nc.scalar.activation(
+                z_grouped[u][:, :, t],
+                lifted[t][:].rearrange("p (m u) -> p u m", u=PACK)[:, u, :],
+                COPY,
+                scale=gains[:, t : t + 1],
+            )
+
         lifted = []
         for t in range(PACK):
             neg_pa = tile("neg_pa%d" % t, [P, W], F32)
@@ -186,40 +205,21 @@ def tile_picked_valliftpagex_none_po_kernel(
             nc.vector.tensor_tensor(dt[:].indirect(n1_list[:]), pb[:], neg_pa[:], ALU.add)
             nc.vector.tensor_copy(dt[:].indirect(n2_list[:]), rb[:])
             lifted.append(dt)
-            if t < PACK - 1:
-                nc.scalar.activation(
-                    z_grouped[:, :, :, t].rearrange("p u m -> p m u"),
-                    dt[:].rearrange("p (m u) -> p m u", u=PACK),
-                    COPY,
-                    scale=gains[:, t : t + 1],
-                )
+            if t < last:
+                for u in range(PACK):
+                    round_z(t, u)
 
-        z2_codes = tile("z2_codes", [P, V], U32)
+        z2_codes = tile("z2_codes", [P, V], U32, tag="rb%d" % last)
         z2_scales = tile("z2_scales", [P, V], U8)
         quantize(z2_codes[:], z2_scales[:], z2_grouped[:].rearrange("p v t -> p (v t)"))
 
-        held_early = tile("held_early", [P, 2, V], F32, tag="rb%d" % (PACK - 1))
-        held_late = tile("held_late", [P, 2, V], F32)
-        held = [held_early[:, 0, :], held_early[:, 1, :], held_late[:, 0, :], held_late[:, 1, :]]
+        scores = []
 
-        def fetch_held(u):
-            nc.vector.tensor_scalar(held[u], page[u][:].indirect(n3_list[:]), 0.5, 0.0, ALU.mult, ALU.add)
-
-        fetch_held(0)
-        fetch_held(1)
-
-        last = PACK - 1
-        s_acc = []
-        for u in range(PACK):
-            nc.scalar.activation(
-                z_grouped[:, u, :, last],
-                lifted[last][:].rearrange("p (m u) -> p u m", u=PACK)[:, u, :],
-                COPY,
-                scale=gains[:, last : last + 1],
-            )
+        def score_product(u):
+            round_z(last, u)
             z_codes = tile("z_codes%d" % u, [P, P], U32)
             z_scales = tile("z_scales%d" % u, [P, P], U8)
-            quantize(z_codes[:], z_scales[:], z_grouped[:, u].rearrange("p m t -> p (m t)"))
+            quantize(z_codes[:], z_scales[:], z_grouped[u][:].rearrange("p m t -> p (m t)"))
             acc = bank(u, "s_acc%d" % u, [P, V])
             nc.tensor.matmul_mx(
                 out=acc[:],
@@ -230,42 +230,66 @@ def tile_picked_valliftpagex_none_po_kernel(
                 start=True,
                 stop=True,
             )
-            s_acc.append(acc)
+            return acc
 
-        z3_grouped = [tile("z3_grouped%d" % c, [P, width, PACK], BF16) for c, width in enumerate(CHUNKS)]
+        def score_rows(u, acc):
+            score = tile("score%d" % u, [P, V], F32)
+            nc.scalar.activation(score[:], acc[:], COPY, scale=0.0625)
+            scores.append(score)
+
+        s_acc = [score_product(u) for u in range(last)]
+        score_rows(0, s_acc[0])
+        s_acc.append(score_product(last))
+        for u in range(1, PACK):
+            score_rows(u, s_acc[u])
+
+        leads = []
         for u in range(PACK):
-            if u >= 2:
-                fetch_held(u)
-            nw = tile("nw%d" % u, [P, V], F32)
-            nc.vector.scalar_tensor_tensor(nw[:], s_acc[u][:], 0.0625, held[u], ALU.mult, ALU.max)
-            nc.vector.tensor_copy(page[u][:].indirect(n3_list[:]), nw[:])
-            if u == 0:
-                w3_dealt = deal_by_ones("w3_dealt", w3_raw, 2)
-                w3_dealt_scales = deal_by_ones("w3_dealt_scales", raw_scales[2], 1)
-            for c, width in enumerate(CHUNKS):
+            lead = tile("lead%d" % u, [P, V], F32)
+            nc.vector.tensor_tensor(lead[:], half_page[u][:].indirect(n3_list[:]), scores[u][:], ALU.subtract)
+            leads.append(lead)
+        excess = []
+        for u in range(PACK):
+            above = tile("excess%d" % u, [P, V], F32)
+            nc.scalar.activation(above[:], leads[u][:], RELU)
+            excess.append(above)
+
+        z3_starts = [sum(Z3_CHUNKS[:c]) for c in range(len(Z3_CHUNKS))]
+        z3_grouped = [tile("z3_grouped%d" % c, [P, width, PACK], BF16) for c, width in enumerate(Z3_CHUNKS)]
+        for u in range(PACK):
+            nc.vector.tensor_tensor(page[u][:].indirect(n3_list[:]), scores[u][:], excess[u][:], ALU.add)
+            for c, width in enumerate(Z3_CHUNKS):
                 nc.scalar.activation(
                     z3_grouped[c][:, :, u],
-                    page[u][:, starts[c] : starts[c] + width],
+                    page[u][:, z3_starts[c] : z3_starts[c] + width],
                     COPY,
                     scale=gt_cols[:, u : u + 1],
                 )
+        w3_dealt = deal_by_ones("w3_dealt", w3_raw, 2, "score%d" % last)
+        w3_dealt_scales = deal_by_ones("w3_dealt_scales", raw_scales[2], 1, "excess%d" % last)
 
+        z3_planes = {}
         out_codes = tile("out_codes", [P, U], U32)
         out_scales = tile("out_scales", [P, U], U8)
         out_words = out_1[0].rearrange("p n t -> p (n t)").bitcast(I32)
         next_bank = PACK
         for c, width in enumerate(CHUNKS):
             cols = slice(starts[c], starts[c] + width)
-            z3_codes = tile("z3_codes%d" % c, [P, width], U32)
-            z3_scales = tile("z3_scales%d" % c, [P, width], U8)
-            quantize(z3_codes[:], z3_scales[:], z3_grouped[c][:].rearrange("p w t -> p (w t)"))
+            source = max(i for i, s in enumerate(z3_starts) if s <= starts[c])
+            if source not in z3_planes:
+                z3_codes = tile("z3_codes%d" % source, [P, Z3_CHUNKS[source]], U32)
+                z3_scales = tile("z3_scales%d" % source, [P, Z3_CHUNKS[source]], U8)
+                quantize(z3_codes[:], z3_scales[:], z3_grouped[source][:].rearrange("p w t -> p (w t)"))
+                z3_planes[source] = (z3_codes, z3_scales)
+            inside = slice(starts[c] - z3_starts[source], starts[c] - z3_starts[source] + width)
+            z3_codes, z3_scales = z3_planes[source]
             result = tile("result%d" % c, [P, PACK, width], F32)
             per_bank = 512 // width
             for first in range(0, PACK, per_bank):
                 acc = bank(next_bank % 8, "out_acc%d_%d" % (c, first), [P, per_bank, width])
                 next_bank = next_bank + 1
                 for j in range(per_bank):
-                    weight_pass(acc[:, j, :], w3_dealt, w3_dealt_scales, first + j, z3_codes[:], z3_scales[:])
+                    weight_pass(acc[:, j, :], w3_dealt, w3_dealt_scales, first + j, z3_codes[:, inside], z3_scales[:, inside])
                 nc.vector.tensor_tensor(
                     result[:, first : first + per_bank, :], acc[:], residual[c][:, first : first + per_bank, :], ALU.add
                 )

from contextlib import ExitStack

import concourse.mybir as mybir
from concourse.masks import make_identity

K, T, S, V, N, H, W, U = 512, 2048, 512, 512, 512, 512, 256, 1024
FLOPS = 2 * (K * H * S + K * H * V + H * S * V + S * N * U)

F32 = mybir.dt.float32
BF16 = mybir.dt.bfloat16
I32 = mybir.dt.int32
U32 = mybir.dt.uint32
U16 = mybir.dt.uint16
U8 = mybir.dt.uint8
FP8X4 = mybir.dt.float8_e4m3fn_x4
FP4X4 = mybir.dt.float4_e2m1fn_x4
ALU = mybir.AluOpType
COPY = mybir.ActivationFunctionType.Copy
RELU = mybir.ActivationFunctionType.Relu

P = 128
PACK = 4
CHUNKS = (128, 128, 256, 256, 128, 128)
Z3_CHUNKS = (128, 128, 256, 256, 256)
VECTOR_ROUNDS_FROM = 5
EARLY_CODES = 3


def tile_picked_valliftpagex_none_po_kernel(
    tc, x_words, x_scales, w1_words, w1_scales, w2_words, w2_scales, ga, gb, mem, gt, res,
    w3_words, w3_scales, offs, two, n1, n2, n3, out_0, out_1, out_2
):
    nc = tc.nc
    with ExitStack() as ctx:
        lists = ctx.enter_context(tc.tile_pool(name="lists", bufs=1))
        sb = ctx.enter_context(tc.tile_pool(name="sb", bufs=1))
        psum = ctx.enter_context(tc.psum_pool(name="psum", bufs=1))

        def tile(name, shape, dtype, tag=None):
            return sb.tile(shape, dtype, name=name, tag=tag or name, align_bytes=64)

        def bank(index, name, shape):
            return psum.tile(shape, F32, name=name, tag="bank%d" % index)

        def load_list(name, source):
            held = lists.tile([P, source.shape[1]], U16, name=name)
            nc.sync.dma_start(held[:], source)
            return held

        def load_scale_rows(plane, source):
            for quad in range(4):
                nc.sync.dma_start(
                    plane[32 * quad : 32 * quad + 4, :].bitcast(I32),
                    source[0, 4 * quad : 4 * quad + 4, :].bitcast(I32),
                )

        def load_fp4_words(name, source):
            held = tile(name, [P, 2 * H], U8)
            nc.sync.dma_start(held[:].bitcast(I32), source[0].bitcast(I32))
            return held

        x_scale_table = tile("x_scale_table", [P, T], U8)
        nc.vector.memset(x_scale_table[:].bitcast(I32)[:, 0:352], 0)
        nc.gpsimd.memset(x_scale_table[:].bitcast(I32)[:, 352:512], 0)
        raw_scales = []
        for i in range(3):
            plane = tile("raw_scales%d" % i, [P, H], U8)
            (nc.vector if i == 0 else nc.gpsimd).memset(plane[:].bitcast(I32), 0)
            raw_scales.append(plane)
        identity = tile("identity", [P, P], F32)
        gain_rows = tile("gain_rows", [P, P], F32)
        nc.gpsimd.memset(gain_rows[:], 0.0)
        make_identity(nc, identity[:])

        offs_list = load_list("offs_list", offs)
        two_list = load_list("two_list", two)
        w1_raw = load_fp4_words("w1_raw", w1_words)
        load_scale_rows(x_scale_table, x_scales)
        x_word_table = tile("x_word_table", [P, T], I32)
        nc.sync.dma_start(x_word_table[:], x_words[0].rearrange("p n t -> p (n t)").bitcast(I32))
        load_scale_rows(raw_scales[0], w1_scales)
        n1_list = load_list("n1_list", n1)
        n2_list = load_list("n2_list", n2)
        w2_raw = load_fp4_words("w2_raw", w2_words)
        load_scale_rows(raw_scales[1], w2_scales)
        for i, gain in enumerate((ga, gb)):
            nc.sync.dma_start(
                gain_rows[4 * i : 4 * i + 4, :].rearrange("t (q r) -> t q r", r=8),
                gain.rearrange("(q t r) o -> t q (r o)", t=PACK, r=8),
            )
        n3_list = load_list("n3_list", n3)
        mem_rows = mem.rearrange("(p t) w -> t p w", t=PACK)
        page = []
        for t in range(PACK):
            rows = tile("page%d" % t, [P, U], F32)
            nc.sync.dma_start(rows[:], mem_rows[t])
            page.append(rows)
        gt_cols = tile("gt_cols", [P, PACK], F32)
        nc.sync.dma_start(gt_cols[:], gt.rearrange("(p t) o -> p (t o)", t=PACK))
        w3_raw = load_fp4_words("w3_raw", w3_words)
        load_scale_rows(raw_scales[2], w3_scales)
        res_rows = res.rearrange("(p t) w -> p t w", t=PACK)
        out_rows = out_0.rearrange("(p t) w -> p t w", t=PACK)
        starts = [sum(CHUNKS[:c]) for c in range(len(CHUNKS))]
        residual = []
        for c, width in enumerate(CHUNKS):
            part = tile("residual%d" % c, [P, PACK, width], F32)
            nc.sync.dma_start(part[:], res_rows[:, :, starts[c] : starts[c] + width])
            residual.append(part)

        def pick_scales(name, offsets):
            picked = tile(name, [P, S], U8)
            nc.vector.tensor_copy(picked[:], x_scale_table[:].indirect(offsets[:]))
            return picked

        def pick_words(name, offsets):
            picked = tile(name, [P, S], U32)
            nc.vector.tensor_copy(picked[:], x_word_table[:].bitcast(U32).indirect(offsets[:]))
            return picked

        def deal_by_eights(name, raw, run):
            dealt = tile(name, list(raw.shape), U8)
            nc.gpsimd.tensor_copy(
                dealt[:].bitcast(I32).rearrange("p (t q r) -> p t q r", t=PACK, r=run),
                raw[:].bitcast(I32).rearrange("p (q t r) -> p t q r", t=PACK, r=run),
            )
            return dealt

        def deal_by_ones(name, raw, run, tag):
            dealt = tile(name, list(raw.shape), U8, tag=tag)
            nc.vector.tensor_copy(
                dealt[:].rearrange("p (t m r) -> p t m r", t=PACK, r=run),
                raw[:].rearrange("p (m t r) -> p t m r", t=PACK, r=run),
            )
            return dealt

        def weight_pass(acc, words, scales, t, codes, code_scales):
            nc.tensor.matmul_mx(
                out=acc,
                lhsT=words[:, 2 * P * t : 2 * P * (t + 1)].bitcast(FP4X4),
                lhsT_scale=scales[:, P * t : P * (t + 1)],
                rhs=codes.bitcast(FP8X4),
                rhs_scale=code_scales,
                start=True,
                stop=True,
            )

        def quantize(codes, scales, grouped):
            nc.vector.quantize_mx(out=codes.bitcast(FP8X4), scales=scales, in_=grouped)

        xa_scales = pick_scales("xa_scales", offs_list)
        xb_scales = pick_scales("xb_scales", two_list)
        w1_dealt = deal_by_eights("w1_dealt", w1_raw, 4)
        xa_words = pick_words("xa_words", offs_list)
        w1_dealt_scales = deal_by_eights("w1_dealt_scales", raw_scales[0], 2)
        xb_words = pick_words("xb_words", two_list)
        w2_dealt = deal_by_eights("w2_dealt", w2_raw, 4)
        w2_dealt_scales = deal_by_eights("w2_dealt_scales", raw_scales[1], 2)

        a_rows = []
        for t in range(PACK):
            acc = bank(t, "a_acc%d" % t, [P, S])
            weight_pass(acc[:], w1_dealt, w1_dealt_scales, t, xa_words[:], xa_scales[:])
            rows = tile("a_rows%d" % t, [P, S], F32)
            nc.scalar.activation(rows[:], acc[:], COPY)
            a_rows.append(rows)

        turned = bank(7, "turned", [P, P])
        nc.tensor.transpose(turned[:], gain_rows[:], identity[:])
        gains = tile("gains", [P, 2 * PACK], F32)
        nc.scalar.activation(gains[:], turned[:, 0 : 2 * PACK], COPY)

        z2_grouped = tile("z2_grouped", [P, V, PACK], BF16)
        for t in range(PACK):
            acc = bank(PACK + t, "b_acc%d" % t, [P, V])
            weight_pass(acc[:], w2_dealt, w2_dealt_scales, t, xb_words[:], xb_scales[:])
            nc.scalar.activation(z2_grouped[:, :, t], acc[:], COPY, scale=gains[:, PACK + t : PACK + t + 1])

        half_page = []
        for u in range(PACK):
            half = tile("half_page%d" % u, [P, U], F32)
            nc.scalar.activation(half[:], page[u][:], COPY, scale=0.5)
            half_page.append(half)

        last = PACK - 1
        z_grouped = [tile("z_grouped%d" % u, [P, P, PACK], BF16) for u in range(PACK)]

        def round_z(t, u):
            nc.scalar.activation(
                z_grouped[u][:, :, t],
                lifted[t][:].rearrange("p (m u) -> p u m", u=PACK)[:, u, :],
                COPY,
                scale=gains[:, t : t + 1],
            )

        lifted = []
        for t in range(PACK):
            neg_pa = tile("neg_pa%d" % t, [P, W], F32)
            pb = tile("pb%d" % t, [P, W], F32)
            rb = tile("rb%d" % t, [P, W], F32)
            dt = tile("dt%d" % t, [P, S], F32)
            nc.vector.tensor_scalar(neg_pa[:], a_rows[t][:].indirect(n1_list[:]), -1.0, 0.0, ALU.mult, ALU.add)
            nc.vector.tensor_copy(pb[:], a_rows[t][:].indirect(n2_list[:]))
            nc.vector.scalar_tensor_tensor(rb[:], neg_pa[:], -0.5, pb[:], ALU.mult, ALU.max)
            nc.vector.tensor_tensor(dt[:].indirect(n1_list[:]), pb[:], neg_pa[:], ALU.add)
            nc.vector.tensor_copy(dt[:].indirect(n2_list[:]), rb[:])
            lifted.append(dt)
            if t < last:
                for u in range(PACK):
                    round_z(t, u)

        z2_codes = tile("z2_codes", [P, V], U32, tag="rb%d" % last)
        z2_scales = tile("z2_scales", [P, V], U8)
        quantize(z2_codes[:], z2_scales[:], z2_grouped[:].rearrange("p v t -> p (v t)"))

        scores = []

        def score_product(u):
            round_z(last, u)
            z_codes = tile("z_codes%d" % u, [P, P], U32)
            z_scales = tile("z_scales%d" % u, [P, P], U8)
            quantize(z_codes[:], z_scales[:], z_grouped[u][:].rearrange("p m t -> p (m t)"))
            acc = bank(u, "s_acc%d" % u, [P, V])
            nc.tensor.matmul_mx(
                out=acc[:],
                lhsT=z_codes[:].bitcast(FP8X4),
                lhsT_scale=z_scales[:],
                rhs=z2_codes[:].bitcast(FP8X4),
                rhs_scale=z2_scales[:],
                start=True,
                stop=True,
            )
            return acc

        def score_rows(u, acc):
            score = tile("score%d" % u, [P, V], F32)
            nc.scalar.activation(score[:], acc[:], COPY, scale=0.0625)
            scores.append(score)

        s_acc = [score_product(u) for u in range(last)]
        score_rows(0, s_acc[0])
        s_acc.append(score_product(last))
        for u in range(1, PACK):
            score_rows(u, s_acc[u])

        leads = []
        for u in range(PACK):
            lead = tile("lead%d" % u, [P, V], F32)
            nc.vector.tensor_tensor(lead[:], half_page[u][:].indirect(n3_list[:]), scores[u][:], ALU.subtract)
            leads.append(lead)
        excess = []
        for u in range(PACK):
            above = tile("excess%d" % u, [P, V], F32)
            nc.scalar.activation(above[:], leads[u][:], RELU)
            excess.append(above)

        z3_starts = [sum(Z3_CHUNKS[:c]) for c in range(len(Z3_CHUNKS))]
        z3_grouped = [tile("z3_grouped%d" % c, [P, width, PACK], BF16) for c, width in enumerate(Z3_CHUNKS)]
        for u in range(PACK):
            nc.vector.tensor_tensor(page[u][:].indirect(n3_list[:]), scores[u][:], excess[u][:], ALU.add)
            for c, width in enumerate(Z3_CHUNKS):
                nc.scalar.activation(
                    z3_grouped[c][:, :, u],
                    page[u][:, z3_starts[c] : z3_starts[c] + width],
                    COPY,
                    scale=gt_cols[:, u : u + 1],
                )
        w3_dealt = deal_by_ones("w3_dealt", w3_raw, 2, "score%d" % last)
        w3_dealt_scales = deal_by_ones("w3_dealt_scales", raw_scales[2], 1, "excess%d" % last)

        z3_planes = {}
        out_codes = tile("out_codes", [P, U], U32)
        out_scales = tile("out_scales", [P, U], U8)
        out_words = out_1[0].rearrange("p n t -> p (n t)").bitcast(I32)
        next_bank = PACK
        for c, width in enumerate(CHUNKS):
            cols = slice(starts[c], starts[c] + width)
            source = max(i for i, s in enumerate(z3_starts) if s <= starts[c])
            if source not in z3_planes:
                z3_codes = tile("z3_codes%d" % source, [P, Z3_CHUNKS[source]], U32)
                z3_scales = tile("z3_scales%d" % source, [P, Z3_CHUNKS[source]], U8)
                quantize(z3_codes[:], z3_scales[:], z3_grouped[source][:].rearrange("p w t -> p (w t)"))
                z3_planes[source] = (z3_codes, z3_scales)
            inside = slice(starts[c] - z3_starts[source], starts[c] - z3_starts[source] + width)
            z3_codes, z3_scales = z3_planes[source]
            result = tile("result%d" % c, [P, PACK, width], F32)
            per_bank = 512 // width
            for first in range(0, PACK, per_bank):
                acc = bank(next_bank % 8, "out_acc%d_%d" % (c, first), [P, per_bank, width])
                next_bank = next_bank + 1
                for j in range(per_bank):
                    weight_pass(acc[:, j, :], w3_dealt, w3_dealt_scales, first + j, z3_codes[:, inside], z3_scales[:, inside])
                nc.vector.tensor_tensor(
                    result[:, first : first + per_bank, :], acc[:], residual[c][:, first : first + per_bank, :], ALU.add
                )
            nc.sync.dma_start(out_rows[:, :, cols], result[:])
            out_grouped = tile("out_grouped%d" % c, [P, width, PACK], BF16)
            if c < VECTOR_ROUNDS_FROM:
                nc.scalar.copy(
                    out_grouped[:].rearrange("p (g i) t -> p g t i", i=4),
                    result[:].rearrange("p t (g i) -> p g t i", i=4),
                )
            else:
                nc.vector.tensor_copy(
                    out_grouped[:].rearrange("p (g i) t -> p g t i", i=4),
                    result[:].rearrange("p t (g i) -> p g t i", i=4),
                )
            quantize(out_codes[:, cols], out_scales[:, cols], out_grouped[:].rearrange("p w t -> p (w t)"))
            if c == EARLY_CODES - 1:
                nc.sync.dma_start(out_words[:, 0 : cols.stop], out_codes[:, 0 : cols.stop].bitcast(I32))
        late = slice(starts[EARLY_CODES], U)
        nc.sync.dma_start(out_words[:, late], out_codes[:, late].bitcast(I32))
        for quad in range(4):
            (nc.sync if quad % 2 else nc.scalar).dma_start(
                out_2[0, 4 * quad : 4 * quad + 4, :].bitcast(I32),
                out_scales[32 * quad : 32 * quad + 4, :].bitcast(I32),
            )
